import numpy as np
import ml_dtypes


def mxq(x, axis, fmt="e4m3"):
    dtype, down = {"e4m3": (ml_dtypes.float8_e4m3fn, 7), "e5m2": (ml_dtypes.float8_e5m2, 14)}[fmt]
    v = np.moveaxis(np.asarray(x, np.float32).astype(ml_dtypes.bfloat16).astype(np.float64), axis, -1)
    blocks = v.reshape(v.shape[:-1] + (-1, 32))
    amax = np.abs(blocks).max(-1, keepdims=True)
    byte = np.maximum(np.where(amax > 0, np.frexp(amax)[1] - 1 + 127, 0) - down, 1)
    scale = np.exp2(byte - 127.0)
    codes = (blocks / scale).astype(np.float32).astype(dtype).astype(np.float64)
    return np.moveaxis((codes * scale).reshape(v.shape), -1, axis)


WIDE = False


def mx_kscale(k):
    if not WIDE:
        return np.ones(k)
    levels = np.array([10, -10, 5, -5, 0])
    if k % 512:
        return np.exp2(np.random.permutation(np.resize(levels, k // 32))).repeat(32)
    a = np.empty((k // 512, 16))
    for p in range(k // 512):
        a[p, :8] = np.random.permutation(np.resize(levels, 8))
        for g in range(8):
            far = levels[np.abs(levels - a[p, g]) >= 10]
            a[p, g + 8] = far[np.random.randint(len(far))]
    return np.exp2(a.ravel()).repeat(32)


BF16 = ml_dtypes.bfloat16


def bf(x):
    return np.asarray(x, np.float32).astype(BF16)


def f64(x):
    return np.asarray(x).astype(np.float64)


E2M1 = np.array([0.0, 0.5, 1.0, 1.5, 2.0, 3.0, 4.0, 6.0, -0.0, -0.5, -1.0, -1.5, -2.0, -3.0, -4.0, -6.0])


def pack_weight(w, fmt):
    k, n = w.shape
    w = f64(bf(w)).reshape(k // 32, 32, n)
    amax = np.abs(w).max(1)
    if fmt == "e4m3":
        byte = np.frexp(amax)[1] - 1 + 127 - 7
    else:
        mant, ex = np.frexp(amax / 6.0)
        byte = np.where(mant > 0.5, ex, ex - 1) + 127
    byte = np.clip(np.where(amax > 0, byte, 1), 1, 254)
    scaled = (w * np.exp2(127.0 - byte)[:, None, :]).reshape(k, n).astype(np.float32)
    by_word = np.ascontiguousarray(scaled.reshape(k // 512, 128, 4, n).transpose(0, 1, 3, 2))
    if fmt == "e4m3":
        words = by_word.astype(ml_dtypes.float8_e4m3fn).view(np.uint8)
    else:
        c = by_word.astype(ml_dtypes.float4_e2m1fn).view(np.uint8) & 0xF
        words = c[..., 0::2] | (c[..., 1::2] << 4)
    return np.ascontiguousarray(words), np.ascontiguousarray(byte.astype(np.uint8).reshape(k // 512, 16, n))


def unpack_weight(words, scales, fmt):
    g, p, n, _ = words.shape
    if fmt == "e4m3":
        vals = np.ascontiguousarray(words).view(ml_dtypes.float8_e4m3fn).astype(np.float64)
    else:
        nib = np.empty((g, p, n, 4), np.uint8)
        nib[..., 0::2] = words & 0xF
        nib[..., 1::2] = words >> 4
        vals = E2M1[nib]
    vals = vals * np.repeat(np.exp2(scales.astype(np.float64) - 127.0), 8, axis=1)[..., None]
    return vals.transpose(0, 1, 3, 2).reshape(g * 512, n)

def planes(Y):
    n, m = Y.shape
    b = f64(bf(Y)).reshape(n // 32, 32, m)
    amax = np.abs(b).max(1)
    byte = np.clip(np.where(amax > 0, np.frexp(amax)[1] - 1 + 127 - 7, 1), 1, 254)
    codes = (b * np.exp2(127.0 - byte)[:, None, :]).reshape(n, m).astype(np.float32).astype(ml_dtypes.float8_e4m3fn).view(np.uint8)
    words = codes.reshape(n // 512, 128, 4, m).transpose(0, 1, 3, 2)
    return np.ascontiguousarray(words), np.ascontiguousarray(byte.astype(np.uint8).reshape(n // 512, 16, m))


B, L, D, F, DO = 2, 1024, 1024, 1024, 1024
BLOCKS = (1, 2, 4, 8)


def block_mean_repeat(h, b):
    if b == 1:
        return h
    n, length, f = h.shape
    means = np.mean(h.reshape(n, length // b, b, f), axis=2)
    return np.repeat(means, b, axis=1)


def softmax_last(v):
    e = np.exp(v - v.max(axis=-1, keepdims=True))
    return e / e.sum(axis=-1, keepdims=True)


def setup_inputs():
    s, t = mx_kscale(D), mx_kscale(F)
    x = bf(np.random.standard_normal((B, L, D)) * s)
    w1_words, w1_scales = pack_weight(np.random.standard_normal((D, F)) / np.sqrt(D) / s[:, None] * t, "e4m3")
    b1 = bf(np.random.standard_normal(F) * 0.3 * t)
    ws = bf(2.0 * np.random.standard_normal(F) / np.sqrt(F) / t)
    w2_words, w2_scales = pack_weight(1.5 * np.random.standard_normal((F, DO)) / np.sqrt(F) / t[:, None], "e4m3")
    return {"x": x,
            "w1_words": w1_words,
            "w1_scales": w1_scales,
            "b1": b1,
            "ws": ws,
            "w2_words": w2_words,
            "w2_scales": w2_scales}


def core(x, w1_words, w1_scales, b1, ws, w2_words, w2_scales):
    h = (mxq(f64(x), 2, "e4m3") @ unpack_weight(w1_words, w1_scales, "e4m3")) + f64(b1)
    wsf = f64(ws)

    cands = []
    scores = []
    for b in BLOCKS:
        p = block_mean_repeat(h, b)
        cands.append(p)
        scores.append(np.sum(p * wsf, axis=-1))
    sc = np.stack(scores, axis=-1)

    a = softmax_last(sc)

    m = np.zeros_like(h)
    for i, p in enumerate(cands):
        m = m + a[:, :, i, None] * p

    d = 0.5 * (m[:, 0::2, :] + m[:, 1::2, :])

    return mxq(d, 2, "e4m3") @ unpack_weight(w2_words, w2_scales, "e4m3")


def reference(x, w1_words, w1_scales, b1, ws, w2_words, w2_scales):
    R_out = core(x, w1_words, w1_scales, b1, ws, w2_words, w2_scales)
    words, scales = planes(np.moveaxis(R_out, 1, 0).reshape(512, -1))
    return R_out, words, scales

@@ -1,0 +1,371 @@
+from contextlib import ExitStack
+
+import concourse.mybir as mybir
+from concourse.masks import make_identity
+
+F32 = mybir.dt.float32
+BF16 = mybir.dt.bfloat16
+U32 = mybir.dt.uint32
+I32 = mybir.dt.int32
+U8 = mybir.dt.uint8
+FP8X4 = mybir.dt.float8_e4m3fn_x4
+MULT = mybir.AluOpType.mult
+ADD = mybir.AluOpType.add
+SUB = mybir.AluOpType.subtract
+MAX = mybir.AluOpType.max
+GE = mybir.AluOpType.is_ge
+AX = mybir.AxisListType.X
+EXP = mybir.ActivationFunctionType.Exp
+
+B, L, D, F, DO = 2, 1024, 1024, 1024, 1024
+P = 128
+NT = B * L // P
+GT = 8
+FLOPS = 2 * B * L * D * F + 2 * B * (L // 2) * F * DO + 2 * 4 * B * L * F
+
+
+def tile_charformersoftsubwordblockmixer_x2_kernel(
+    tc, x, w1_words, w1_scales, b1, ws, w2_words, w2_scales, out_0, out_1, out_2
+):
+    nc = tc.nc
+    with ExitStack() as ctx:
+        keep = ctx.enter_context(tc.tile_pool(name="keep", bufs=1))
+        xin = ctx.enter_context(tc.tile_pool(name="xin", bufs=8))
+        work = ctx.enter_context(tc.tile_pool(name="work", bufs=4))
+        hpool = ctx.enter_context(tc.tile_pool(name="hpool", bufs=16))
+        small = ctx.enter_context(tc.tile_pool(name="small", bufs=2))
+        two = ctx.enter_context(tc.tile_pool(name="two", bufs=2))
+        pmm = ctx.enter_context(tc.psum_pool(name="pmm", bufs=4))
+        pxt = ctx.enter_context(tc.psum_pool(name="pxt", bufs=3))
+        pone = ctx.enter_context(tc.psum_pool(name="pone", bufs=1))
+
+        ctx.enter_context(tc.manual_schedule())
+
+        w1w = keep.tile([P, 2, F], U32, align_bytes=256, name="w1w")
+        w1s = keep.tile([P, 2, F], U8, align_bytes=256, name="w1s")
+        w2w = keep.tile([P, 2, DO], U32, align_bytes=256, name="w2w")
+        w2s = keep.tile([P, 2, DO], U8, align_bytes=256, name="w2s")
+        wsb = keep.tile([P, F], BF16, name="wsb")
+        b1t = keep.tile([P, 2, 4], BF16, name="b1t")
+
+        ident = keep.tile([P, P], F32, name="ident")
+        make_identity(nc, ident[:])
+        nc.vector.memset(w1s[:].bitcast(I32), 0)
+        nc.vector.memset(w2s[:].bitcast(I32), 0)
+        scr = keep.tile([P, 1], F32, name="scr")
+        nc.vector.memset(scr[:], 0.0)
+        scr2 = keep.tile([P, 1], F32, name="scr2")
+        nc.scalar.activation(out=scr2[:], in_=scr[:], func=EXP)
+
+        xt_in = []
+
+        def load_x(pair):
+            t = xin.tile([P, 2, D], BF16, name="xp", align_bytes=256)
+            n, r0 = divmod(pair * 2 * P, L)
+            for e in range(2):
+                nc.sync.dma_start(out=t[:, e, :], in_=x[n, r0 + e * P : r0 + (e + 1) * P, :])
+            xt_in.append(t)
+
+        def load_w(words, tile, c0, c1):
+            v = words.rearrange("g p n t -> p g (n t)")
+            nc.sync.dma_start(
+                out=tile[:, :, c0:c1].bitcast(I32), in_=v[:, :, 4 * c0 : 4 * c1].bitcast(I32)
+            )
+
+        def load_s(scales, tile):
+            for q in range(4):
+                nc.sync.dma_start(
+                    out=tile[32 * q : 32 * q + 4, :, :].bitcast(I32),
+                    in_=scales[:, 4 * q : 4 * q + 4, :].rearrange("g q n -> q g n").bitcast(I32),
+                )
+
+        load_x(0)
+        load_s(w1_scales, w1s)
+        load_w(w1_words, w1w, 0, 512)
+        load_x(1)
+        load_w(w1_words, w1w, 512, 1024)
+        nc.gpsimd.dma_start(out=wsb[:], in_=ws.partition_broadcast(P))
+        nc.gpsimd.dma_start(out=b1t[:], in_=b1.rearrange("(g m t) -> m g t", g=2, t=4))
+        for pair in range(2, 8):
+            load_x(pair)
+        load_s(w2_scales, w2s)
+        load_w(w2_words, w2w, 0, 512)
+        load_w(w2_words, w2w, 512, 1024)
+
+        pool_m = [ident]
+        for b in (2, 4, 8):
+            m = keep.tile([P, P], F32, name="pm%d" % b)
+            nc.gpsimd.memset(m[:], 1.0 / b)
+            pat = [[-b, P // b], [0, b]]
+            nc.gpsimd.affine_select(out=m[:], in_=m[:], compare_op=GE, fill=0.0, base=0, pattern=pat, channel_multiplier=1)
+            pat = [[b, P // b], [0, b]]
+            nc.gpsimd.affine_select(out=m[:], in_=m[:], compare_op=GE, fill=0.0, base=b - 1, pattern=pat, channel_multiplier=-1)
+            pool_m.append(m)
+        e8 = keep.tile([P, P], F32, name="e8")
+        nc.vector.tensor_scalar(out=e8[:], in0=pool_m[3][:], scalar1=4.0, scalar2=None, op0=MULT)
+        wtab = keep.tile([P, 4, 3], F32, name="wtab")
+        for k in range(3):
+            nc.vector.tensor_reduce(
+                out=wtab[:, :, k],
+                in_=pool_m[k + 1][:].rearrange("p (q j e) -> p j e q", j=4, e=2)[:, :, 0, :],
+                axis=AX,
+                op=ADD,
+            )
+        pmask = keep.tile([P, 4], F32, name="pmask")
+        nc.vector.tensor_scalar(out=pmask[:], in0=wtab[:, :, 0], scalar1=2.0, scalar2=None, op0=MULT)
+        bmask = keep.tile([P, 16], F32, name="bmask")
+        nc.vector.tensor_scalar(out=bmask[:], in0=pool_m[3][:, 0:P:8], scalar1=8.0, scalar2=None, op0=MULT)
+
+        xg_t, xq_t, h_t, u_t, ct_t, am_t, a_t, db_t = {}, {}, {}, {}, {}, {}, {}, {}
+
+        def transposes(i):
+            words = xt_in[i // 2][:, i % 2, :].bitcast(F32)
+            xt = pxt.tile([P, 2, 2, P], F32, name="xt", tag="tp")
+            for g in range(2):
+                for u in range(2):
+                    nc.tensor.transpose(xt[:, g, u, :], words[:, 256 * g + u : 256 * (g + 1) : 2], ident[:])
+            xg = work.tile([P, 2, P, 4], BF16, name="xg", align_bytes=256)
+            nc.scalar.copy(out=xg[:].bitcast(F32), in_=xt[:].rearrange("p g u r -> p g r u"))
+            xg_t[i] = xg
+
+        def quant_x(i):
+            xq = work.tile([P, 2, P], U32, name="xq", align_bytes=256)
+            xs = work.tile([P, 2, P], U8, name="xs", align_bytes=256)
+            nc.vector.quantize_mx(
+                out=xq[:].rearrange("p g r -> p (g r)").bitcast(FP8X4),
+                scales=xs[:].rearrange("p g r -> p (g r)"),
+                in_=xg_t[i][:].rearrange("p g r k -> p (g r k)"),
+            )
+            xq_t[i] = (xq, xs)
+
+        def stage1(i):
+            xq, xs = xq_t[i]
+            h = hpool.tile([P, 2, 4, P], F32, name="h", align_bytes=256)
+            h_t[i] = h
+            if i % GT == 0:
+                u_t[i // GT] = small.tile([P, GT, 2], F32, name="u")
+            for half in range(2):
+                cols = slice(512 * half, 512 * (half + 1))
+                acc = pmm.tile([P, 512], F32, name="mm")
+                for g in range(2):
+                    nc.tensor.matmul_mx(
+                        out=acc[:],
+                        lhsT=xq[:, g, :].bitcast(FP8X4),
+                        lhsT_scale=xs[:, g, :],
+                        rhs=w1w[:, g, cols].bitcast(FP8X4),
+                        rhs_scale=w1s[:, g, cols],
+                        start=(g == 0),
+                        stop=(g == 1),
+                    )
+                prod = work.tile([P, 512], F32, name="prod")
+                nc.vector.scalar_tensor_tensor(
+                    out=prod[:], in0=acc[:], scalar=1.0, in1=wsb[:, cols], op0=MULT, op1=MULT,
+                    accum_out=u_t[i // GT][:, i % GT, half : half + 1],
+                )
+                nc.scalar.copy(out=h[:, half], in_=acc[:].rearrange("p (m k) -> p k m", k=4))
+
+        def scores_pe(G):
+            sp = pone.tile([P, 4, GT, 2], F32, name="sp", tag="sm")
+            for b in range(4):
+                nc.tensor.matmul(
+                    out=sp[:, b].rearrange("p i h -> p (i h)"),
+                    lhsT=pool_m[b][:],
+                    rhs=u_t[G][:].rearrange("p i h -> p (i h)"),
+                    start=True,
+                    stop=True,
+                )
+            return sp
+
+        def softmax(G, sp):
+            sc = small.tile([P, 4, GT], F32, name="sc")
+            nc.vector.tensor_reduce(out=sc[:], in_=sp[:], axis=AX, op=ADD)
+            mx = small.tile([P, GT], F32, name="mx")
+            nc.vector.tensor_reduce(out=mx[:], in_=sc[:].rearrange("p b i -> p i b"), axis=AX, op=MAX)
+            sd = small.tile([P, 4, GT], F32, name="sd")
+            nc.vector.tensor_tensor(
+                out=sd[:], in0=sc[:], in1=mx[:].unsqueeze(1).to_broadcast([P, 4, GT]), op=SUB
+            )
+            ex = small.tile([P, 4, GT], F32, name="ex")
+            nc.scalar.activation(out=ex[:], in_=sd[:], func=EXP)
+            sm = small.tile([P, GT], F32, name="sm")
+            nc.vector.tensor_reduce(out=sm[:], in_=ex[:].rearrange("p b i -> p i b"), axis=AX, op=ADD)
+            rc = small.tile([P, GT], F32, name="rc")
+            nc.vector.reciprocal(out=rc[:], in_=sm[:])
+            a = small.tile([P, 4, GT], F32, name="a")
+            nc.vector.tensor_tensor(
+                out=a[:], in0=ex[:], in1=rc[:].unsqueeze(1).to_broadcast([P, 4, GT]), op=MULT
+            )
+            am = small.tile([P, 4, 3 * GT], F32, name="am")
+            nc.vector.tensor_tensor(
+                out=am[:],
+                in0=a[:, 1:4, :].rearrange("p b i -> p (b i)").unsqueeze(1).to_broadcast([P, 4, 3 * GT]),
+                in1=pmask[:].unsqueeze(2).to_broadcast([P, 4, 3 * GT]),
+                op=MULT,
+            )
+            a_t[G], am_t[G] = a, am
+
+        def coef(G):
+            cp = pone.tile([P, 4, 3, GT], F32, name="cp", tag="sm")
+            nc.tensor.matmul(
+                out=cp[:].rearrange("p j b i -> p (j b i)"),
+                lhsT=e8[:],
+                rhs=am_t[G][:].rearrange("p j c -> p (j c)"),
+                start=True,
+                stop=True,
+            )
+            tmp = small.tile([P, GT, 4, 4], F32, name="tmp")
+            for k in range(3):
+                nc.vector.tensor_tensor(
+                    out=tmp[:, :, :, k + 1],
+                    in0=cp[:, :, k, :].rearrange("p j i -> p i j"),
+                    in1=wtab[:, :, k].unsqueeze(1).to_broadcast([P, GT, 4]),
+                    op=MULT,
+                )
+            nc.vector.tensor_tensor(
+                out=tmp[:, :, :, 0],
+                in0=a_t[G][:, 0, :].unsqueeze(2).to_broadcast([P, GT, 4]),
+                in1=wtab[:, :, 0].unsqueeze(1).to_broadcast([P, GT, 4]),
+                op=MULT,
+            )
+            c = small.tile([P, GT * 4], F32, name="c")
+            nc.vector.tensor_reduce(out=c[:], in_=tmp[:].rearrange("p i j b -> p (i j) b"), axis=AX, op=ADD)
+            ct = small.tile([P, GT * 4, 16], F32, name="ct")
+            for k in range(0, GT * 4, 8):
+                nc.gpsimd.tensor_tensor(
+                    out=ct[:, k : k + 8],
+                    in0=c[:, k : k + 8].unsqueeze(2).to_broadcast([P, 8, 16]),
+                    in1=bmask[:].unsqueeze(1).to_broadcast([P, 8, 16]),
+                    op=MULT,
+                )
+            ct_t[G] = ct
+
+        def combine(i):
+            n, il = divmod(i, NT // B)
+            if il == 0:
+                db_t[n] = two.tile([P, 2, 512, 4], BF16, name="db", align_bytes=256)
+            db = db_t[n]
+            ct = ct_t[i // GT]
+            k4 = 4 * (i % GT)
+            dp = pxt.tile([P, 2, 4, 64], F32, name="dp", tag="tp")
+            for g in range(2):
+                for k in range(4):
+                    nc.tensor.matmul(
+                        out=dp[:, g, k, :],
+                        lhsT=h_t[i][:, g, k, :],
+                        rhs=ct[:, k4 : k4 + 4, :].rearrange("p t q -> p (t q)"),
+                        start=True,
+                        stop=True,
+                    )
+            for g in range(2):
+                nc.vector.tensor_tensor(
+                    out=db[:, g].rearrange("p (t c) k -> p t c k", t=4)[:, :, 16 * il : 16 * il + 16, :],
+                    in0=dp[:, g].rearrange("p k (t q) -> p t q k", t=4),
+                    in1=b1t[:, g, :].unsqueeze(1).unsqueeze(1).to_broadcast([P, 4, 16, 4]),
+                    op=ADD,
+                )
+
+        dq_t = {}
+
+        def quant_d(n):
+            dq = two.tile([P, 2, 512], U32, name="dq", align_bytes=256)
+            ds = two.tile([P, 2, 512], U8, name="ds", align_bytes=256)
+            for g in range(2):
+                nc.vector.quantize_mx(
+                    out=dq[:, g, :].bitcast(FP8X4),
+                    scales=ds[:, g, :],
+                    in_=db_t[n][:, g].rearrange("p c k -> p (c k)"),
+                )
+            dq_t[n] = (dq, ds)
+
+        y_t = {}
+
+        def stage2(n, half, t):
+            dq, ds = dq_t[n]
+            cols = slice(512 * half, 512 * (half + 1))
+            if t == 0:
+                y_t[n, half] = two.tile([P, 4, 512], F32, name="yf", align_bytes=256)
+            yf = y_t[n, half]
+            acc = pmm.tile([P, 512], F32, name="mm")
+            rows = slice(P * t, P * (t + 1))
+            for g in range(2):
+                nc.tensor.matmul_mx(
+                    out=acc[:],
+                    lhsT=dq[:, g, rows].bitcast(FP8X4),
+                    lhsT_scale=ds[:, g, rows],
+                    rhs=w2w[:, g, cols].bitcast(FP8X4),
+                    rhs_scale=w2s[:, g, cols],
+                    start=(g == 0),
+                    stop=(g == 1),
+                )
+            nc.scalar.copy(out=yf[:, t, :], in_=acc[:])
+            if t == 3:
+                nc.sync.dma_start(
+                    out=out_0[n].rearrange("(p t) o -> p t o", t=4)[:, :, cols], in_=yf[:]
+                )
+
+        def planes_out(n, half):
+            yf = y_t[n, half]
+            yb = two.tile([P, 512, 4], BF16, name="yb", align_bytes=256)
+            nc.vector.tensor_copy(out=yb[:], in_=yf[:].rearrange("p t o -> p o t"))
+            yq = two.tile([P, 512], U32, name="yq", align_bytes=256)
+            ys = two.tile([P, 512], U8, name="ys", align_bytes=256)
+            nc.vector.quantize_mx(
+                out=yq[:].bitcast(FP8X4), scales=ys[:], in_=yb[:].rearrange("p o t -> p (o t)")
+            )
+            m0 = n * DO + half * 512
+            nc.sync.dma_start(
+                out=out_1[0].rearrange("p m t -> p (m t)")[:, 4 * m0 : 4 * (m0 + 512)].bitcast(I32),
+                in_=yq[:].bitcast(I32),
+            )
+            for q in range(4):
+                nc.sync.dma_start(
+                    out=out_2[0, 4 * q : 4 * q + 4, m0 : m0 + 512].bitcast(I32),
+                    in_=ys[32 * q : 32 * q + 4, :].bitcast(I32),
+                )
+
+        transposes(0)
+        transposes(1)
+        quant_x(0)
+        quant_x(1)
+        for s in range(8):
+            a, b = 2 * s, 2 * s + 1
+            if s < 7:
+                transposes(a + 2)
+                transposes(b + 2)
+            if s == 4:
+                softmax(0, scores_pe(0))
+            stage1(a)
+            if s < 7:
+                quant_x(a + 2)
+            if s >= 5:
+                combine(2 * (s - 5))
+            stage1(b)
+            if s == 4:
+                coef(0)
+            if s < 7:
+                quant_x(b + 2)
+            if 5 <= s < 7:
+                combine(2 * (s - 5) + 1)
+        softmax(1, scores_pe(1))
+        combine(5)
+        combine(6)
+        coef(1)
+        combine(7)
+        quant_d(0)
+        units = [(half, t) for half in range(2) for t in range(4)]
+        combine(8)
+        for half, t in units[:4]:
+            stage2(0, half, t)
+        for i in range(9, 16):
+            combine(i)
+            if i == 11:
+                planes_out(0, 0)
+        quant_d(1)
+        for half, t in units[4:]:
+            stage2(0, half, t)
+        for half in range(2):
+            for t in range(4):
+                stage2(1, half, t)
+            if half == 0:
+                planes_out(0, 1)
+            planes_out(1, half)

@@ -15,12 +15,15 @@ SUB = mybir.AluOpType.subtract
 MAX = mybir.AluOpType.max
 GE = mybir.AluOpType.is_ge
 AX = mybir.AxisListType.X
+AXY = mybir.AxisListType.XY
 EXP = mybir.ActivationFunctionType.Exp
+COPY = mybir.ActivationFunctionType.Copy
 
 B, L, D, F, DO = 2, 1024, 1024, 1024, 1024
 P = 128
-NT = B * L // P
-GT = 8
+NP = 8
+GP = 4
+CW = 256
 FLOPS = 2 * B * L * D * F + 2 * B * (L // 2) * F * DO + 2 * 4 * B * L * F
 
 
@@ -31,8 +34,8 @@ def tile_charformersoftsubwordblockmixer_x2_kernel(
     with ExitStack() as ctx:
         keep = ctx.enter_context(tc.tile_pool(name="keep", bufs=1))
         xin = ctx.enter_context(tc.tile_pool(name="xin", bufs=8))
-        work = ctx.enter_context(tc.tile_pool(name="work", bufs=4))
-        hpool = ctx.enter_context(tc.tile_pool(name="hpool", bufs=16))
+        work = ctx.enter_context(tc.tile_pool(name="work", bufs=3))
+        hpool = ctx.enter_context(tc.tile_pool(name="hpool", bufs=8))
         small = ctx.enter_context(tc.tile_pool(name="small", bufs=2))
         two = ctx.enter_context(tc.tile_pool(name="two", bufs=2))
         pmm = ctx.enter_context(tc.psum_pool(name="pmm", bufs=4))
@@ -46,25 +49,34 @@ def tile_charformersoftsubwordblockmixer_x2_kernel(
         w2w = keep.tile([P, 2, DO], U32, align_bytes=256, name="w2w")
         w2s = keep.tile([P, 2, DO], U8, align_bytes=256, name="w2s")
         wsb = keep.tile([P, F], BF16, name="wsb")
-        b1t = keep.tile([P, 2, 4], BF16, name="b1t")
+        wrow = keep.tile([P, F], BF16, name="wrow")
+        brow = keep.tile([P, F], BF16, name="brow")
+        ones = keep.tile([P, P], BF16, name="ones")
 
         ident = keep.tile([P, P], F32, name="ident")
         make_identity(nc, ident[:])
         nc.vector.memset(w1s[:].bitcast(I32), 0)
-        nc.vector.memset(w2s[:].bitcast(I32), 0)
+        nc.vector.memset(wrow[:], 0.0)
+        nc.vector.memset(brow[:], 0.0)
+        nc.gpsimd.memset(ones[:], 1.0)
+        nc.gpsimd.memset(w2s[:].bitcast(I32), 0)
         scr = keep.tile([P, 1], F32, name="scr")
         nc.vector.memset(scr[:], 0.0)
         scr2 = keep.tile([P, 1], F32, name="scr2")
         nc.scalar.activation(out=scr2[:], in_=scr[:], func=EXP)
 
-        xt_in = []
+        x_t = []
 
-        def load_x(pair):
+        def load_x(c):
             t = xin.tile([P, 2, D], BF16, name="xp", align_bytes=256)
-            n, r0 = divmod(pair * 2 * P, L)
-            for e in range(2):
-                nc.sync.dma_start(out=t[:, e, :], in_=x[n, r0 + e * P : r0 + (e + 1) * P, :])
-            xt_in.append(t)
+            n, cl = divmod(c, NP // B)
+            rows = x[n, 256 * cl : 256 * (cl + 1), :].rearrange("(p e) k -> p e k", e=2)
+            if c == 0:
+                for e in range(2):
+                    nc.sync.dma_start(out=t[:, e, :], in_=rows[:, e, :])
+            else:
+                nc.sync.dma_start(out=t[:], in_=rows)
+            x_t.append(t)
 
         def load_w(words, tile, c0, c1):
             v = words.rearrange("g p n t -> p g (n t)")
@@ -82,68 +94,82 @@ def tile_charformersoftsubwordblockmixer_x2_kernel(
         load_x(0)
         load_s(w1_scales, w1s)
         load_w(w1_words, w1w, 0, 512)
-        load_x(1)
         load_w(w1_words, w1w, 512, 1024)
-        nc.gpsimd.dma_start(out=wsb[:], in_=ws.partition_broadcast(P))
-        nc.gpsimd.dma_start(out=b1t[:], in_=b1.rearrange("(g m t) -> m g t", g=2, t=4))
-        for pair in range(2, 8):
-            load_x(pair)
+        nc.gpsimd.dma_start(out=wrow[0:1, :], in_=ws.unsqueeze(0))
+        load_x(1)
+        nc.gpsimd.dma_start(out=brow[0:1, :], in_=b1.unsqueeze(0))
+        for c in range(2, NP):
+            load_x(c)
         load_s(w2_scales, w2s)
         load_w(w2_words, w2w, 0, 512)
         load_w(w2_words, w2w, 512, 1024)
 
-        pool_m = [ident]
-        for b in (2, 4, 8):
+        pool_m = []
+        for b in (1, 2, 4):
             m = keep.tile([P, P], F32, name="pm%d" % b)
-            nc.gpsimd.memset(m[:], 1.0 / b)
+            nc.gpsimd.memset(m[:], 0.5 / b)
             pat = [[-b, P // b], [0, b]]
             nc.gpsimd.affine_select(out=m[:], in_=m[:], compare_op=GE, fill=0.0, base=0, pattern=pat, channel_multiplier=1)
             pat = [[b, P // b], [0, b]]
             nc.gpsimd.affine_select(out=m[:], in_=m[:], compare_op=GE, fill=0.0, base=b - 1, pattern=pat, channel_multiplier=-1)
             pool_m.append(m)
-        e8 = keep.tile([P, P], F32, name="e8")
-        nc.vector.tensor_scalar(out=e8[:], in0=pool_m[3][:], scalar1=4.0, scalar2=None, op0=MULT)
+        e4 = keep.tile([P, P], F32, name="e4")
         wtab = keep.tile([P, 4, 3], F32, name="wtab")
-        for k in range(3):
-            nc.vector.tensor_reduce(
-                out=wtab[:, :, k],
-                in_=pool_m[k + 1][:].rearrange("p (q j e) -> p j e q", j=4, e=2)[:, :, 0, :],
-                axis=AX,
-                op=ADD,
-            )
         pmask = keep.tile([P, 4], F32, name="pmask")
-        nc.vector.tensor_scalar(out=pmask[:], in0=wtab[:, :, 0], scalar1=2.0, scalar2=None, op0=MULT)
-        bmask = keep.tile([P, 16], F32, name="bmask")
-        nc.vector.tensor_scalar(out=bmask[:], in0=pool_m[3][:, 0:P:8], scalar1=8.0, scalar2=None, op0=MULT)
+        bmask = keep.tile([P, 32], F32, name="bmask")
 
-        xg_t, xq_t, h_t, u_t, ct_t, am_t, a_t, db_t = {}, {}, {}, {}, {}, {}, {}, {}
+        def constants():
+            nc.vector.tensor_scalar(out=e4[:], in0=pool_m[2][:], scalar1=8.0, scalar2=None, op0=MULT)
+            for k in range(3):
+                nc.vector.tensor_reduce(
+                    out=wtab[:, :, k],
+                    in_=pool_m[k][:].rearrange("p (q j) -> p j q", j=4),
+                    axis=AX,
+                    op=ADD,
+                )
+            nc.vector.tensor_scalar(out=pmask[:], in0=wtab[:, :, 0], scalar1=2.0, scalar2=None, op0=MULT)
+            nc.vector.tensor_scalar(out=bmask[:], in0=pool_m[2][:, 0:P:4], scalar1=8.0, scalar2=None, op0=MULT)
 
-        def transposes(i):
-            words = xt_in[i // 2][:, i % 2, :].bitcast(F32)
+        def spread_ws():
+            for half in range(2):
+                cols = slice(512 * half, 512 * (half + 1))
+                acc = pmm.tile([P, 512], F32, name="accw", tag="mm")
+                nc.tensor.matmul(out=acc[:], lhsT=ones[:], rhs=wrow[:, cols], start=True, stop=True)
+                nc.scalar.copy(out=wsb[:, cols], in_=acc[:])
+
+        xg_t, xq_t, he_t, s_t, u_t, mt_t, am_t, kap_t, d_t, db_t, dq_t, y_t = ({}, {}, {}, {}, {}, {}, {}, {}, {}, {}, {}, {})
+
+        def flip(words):
             xt = pxt.tile([P, 2, 2, P], F32, name="xt", tag="tp")
             for g in range(2):
                 for u in range(2):
-                    nc.tensor.transpose(xt[:, g, u, :], words[:, 256 * g + u : 256 * (g + 1) : 2], ident[:])
+                    nc.tensor.transpose(xt[:, g, u, :], words[:, g, u, :], ident[:])
+            return xt
+
+        def flip_x(c, e):
+            xt = flip(x_t[c][:, e, :].bitcast(F32).rearrange("p (g r u) -> p g u r", g=2, u=2))
             xg = work.tile([P, 2, P, 4], BF16, name="xg", align_bytes=256)
             nc.scalar.copy(out=xg[:].bitcast(F32), in_=xt[:].rearrange("p g u r -> p g r u"))
-            xg_t[i] = xg
+            xg_t[c, e] = xg
 
-        def quant_x(i):
+        def quant_x(c, e):
             xq = work.tile([P, 2, P], U32, name="xq", align_bytes=256)
             xs = work.tile([P, 2, P], U8, name="xs", align_bytes=256)
             nc.vector.quantize_mx(
                 out=xq[:].rearrange("p g r -> p (g r)").bitcast(FP8X4),
                 scales=xs[:].rearrange("p g r -> p (g r)"),
-                in_=xg_t[i][:].rearrange("p g r k -> p (g r k)"),
+                in_=xg_t[c, e][:].rearrange("p g r k -> p (g r k)"),
             )
-            xq_t[i] = (xq, xs)
+            xq_t[c, e] = (xq, xs)
 
-        def stage1(i):
-            xq, xs = xq_t[i]
-            h = hpool.tile([P, 2, 4, P], F32, name="h", align_bytes=256)
-            h_t[i] = h
-            if i % GT == 0:
-                u_t[i // GT] = small.tile([P, GT, 2], F32, name="u")
+        def stage1(c, e):
+            xq, xs = xq_t[c, e]
+            if c % GP == 0 and e == 0:
+                u_t[c // GP] = small.tile([P, GP, 2, 2], F32, name="u")
+            u = u_t[c // GP]
+            if e == 0:
+                he_t[c] = hpool.tile([P, 2, 512], F32, name="he", align_bytes=256)
+                s_t[c] = hpool.tile([P, 2, 512], F32, name="s", align_bytes=256)
             for half in range(2):
                 cols = slice(512 * half, 512 * (half + 1))
                 acc = pmm.tile([P, 512], F32, name="mm")
@@ -160,111 +186,134 @@ def tile_charformersoftsubwordblockmixer_x2_kernel(
                 prod = work.tile([P, 512], F32, name="prod")
                 nc.vector.scalar_tensor_tensor(
                     out=prod[:], in0=acc[:], scalar=1.0, in1=wsb[:, cols], op0=MULT, op1=MULT,
-                    accum_out=u_t[i // GT][:, i % GT, half : half + 1],
+                    accum_out=u[:, c % GP, e, half : half + 1],
                 )
-                nc.scalar.copy(out=h[:, half], in_=acc[:].rearrange("p (m k) -> p k m", k=4))
+                if e == 0:
+                    nc.scalar.copy(out=he_t[c][:, half, :], in_=acc[:])
+                else:
+                    nc.scalar.copy(out=s_t[c][:, half, :], in_=acc[:])
 
-        def scores_pe(G):
-            sp = pone.tile([P, 4, GT, 2], F32, name="sp", tag="sm")
-            for b in range(4):
+        def pair_sum(c, halves=(0, 1)):
+            for half in halves:
+                nc.vector.tensor_tensor(
+                    out=s_t[c][:, half, :], in0=s_t[c][:, half, :], in1=he_t[c][:, half, :], op=ADD
+                )
+
+        def scores(G, between):
+            u = u_t[G]
+            sp = pone.tile([P, 3, GP, 2, 2], F32, name="sp", tag="sm")
+            for k in range(3):
                 nc.tensor.matmul(
-                    out=sp[:, b].rearrange("p i h -> p (i h)"),
-                    lhsT=pool_m[b][:],
-                    rhs=u_t[G][:].rearrange("p i h -> p (i h)"),
+                    out=sp[:, k].rearrange("p c e h -> p (c e h)"),
+                    lhsT=pool_m[k][:],
+                    rhs=u[:].rearrange("p c e h -> p (c e h)"),
                     start=True,
                     stop=True,
                 )
-            return sp
-
-        def softmax(G, sp):
-            sc = small.tile([P, 4, GT], F32, name="sc")
-            nc.vector.tensor_reduce(out=sc[:], in_=sp[:], axis=AX, op=ADD)
-            mx = small.tile([P, GT], F32, name="mx")
-            nc.vector.tensor_reduce(out=mx[:], in_=sc[:].rearrange("p b i -> p i b"), axis=AX, op=MAX)
-            sd = small.tile([P, 4, GT], F32, name="sd")
+            lg = small.tile([P, 4, 2, GP], F32, name="lg")
+            nc.vector.tensor_reduce(out=lg[:, 0].rearrange("p e c -> p c e"), in_=u[:], axis=AX, op=ADD)
+            for e in range(2):
+                nc.vector.tensor_reduce(out=lg[:, 1:4, e, :], in_=sp[:], axis=AXY, op=ADD)
+            pair_sum(*between[0])
+            mx = small.tile([P, 2 * GP], F32, name="mx")
+            nc.vector.tensor_reduce(out=mx[:], in_=lg[:].rearrange("p b e c -> p (e c) b"), axis=AX, op=MAX)
+            pair_sum(*between[1])
+            sd = small.tile([P, 4, 2 * GP], F32, name="sd")
             nc.vector.tensor_tensor(
-                out=sd[:], in0=sc[:], in1=mx[:].unsqueeze(1).to_broadcast([P, 4, GT]), op=SUB
+                out=sd[:], in0=lg[:].rearrange("p b e c -> p b (e c)"),
+                in1=mx[:].unsqueeze(1).to_broadcast([P, 4, 2 * GP]), op=SUB,
             )
-            ex = small.tile([P, 4, GT], F32, name="ex")
+            ex = small.tile([P, 4, 2 * GP], F32, name="ex")
             nc.scalar.activation(out=ex[:], in_=sd[:], func=EXP)
-            sm = small.tile([P, GT], F32, name="sm")
-            nc.vector.tensor_reduce(out=sm[:], in_=ex[:].rearrange("p b i -> p i b"), axis=AX, op=ADD)
-            rc = small.tile([P, GT], F32, name="rc")
+            pair_sum(*between[2])
+            sm = small.tile([P, 2 * GP], F32, name="sm")
+            nc.vector.tensor_reduce(out=sm[:], in_=ex[:].rearrange("p b f -> p f b"), axis=AX, op=ADD)
+            pair_sum(*between[3])
+            rc = small.tile([P, 2 * GP], F32, name="rc")
             nc.vector.reciprocal(out=rc[:], in_=sm[:])
-            a = small.tile([P, 4, GT], F32, name="a")
-            nc.vector.tensor_tensor(
-                out=a[:], in0=ex[:], in1=rc[:].unsqueeze(1).to_broadcast([P, 4, GT]), op=MULT
+            a = small.tile([P, 4, 2, GP], F32, name="a")
+            nc.vector.scalar_tensor_tensor(
+                out=a[:].rearrange("p b e c -> p b (e c)"), in0=ex[:], scalar=0.5,
+                in1=rc[:].unsqueeze(1).to_broadcast([P, 4, 2 * GP]), op0=MULT, op1=MULT,
             )
-            am = small.tile([P, 4, 3 * GT], F32, name="am")
+            ks = small.tile([P, 3, GP], F32, name="ks")
+            nc.vector.tensor_tensor(out=ks[:], in0=a[:, 1:4, 0, :], in1=a[:, 1:4, 1, :], op=ADD)
+            kap = small.tile([P, GP], F32, name="kap")
+            nc.vector.tensor_tensor(out=kap[:], in0=a[:, 0, 0, :], in1=a[:, 0, 1, :], op=SUB)
+            nc.vector.scalar_tensor_tensor(
+                out=ks[:, 0, :], in0=a[:, 0, 1, :], scalar=2.0, in1=ks[:, 0, :], op0=MULT, op1=ADD
+            )
+            am = small.tile([P, 4, 3 * GP], F32, name="am")
             nc.vector.tensor_tensor(
                 out=am[:],
-                in0=a[:, 1:4, :].rearrange("p b i -> p (b i)").unsqueeze(1).to_broadcast([P, 4, 3 * GT]),
-                in1=pmask[:].unsqueeze(2).to_broadcast([P, 4, 3 * GT]),
+                in0=ks[:].rearrange("p k c -> p (k c)").unsqueeze(1).to_broadcast([P, 4, 3 * GP]),
+                in1=pmask[:].unsqueeze(2).to_broadcast([P, 4, 3 * GP]),
                 op=MULT,
             )
-            a_t[G], am_t[G] = a, am
+            am_t[G], kap_t[G] = am, kap
 
         def coef(G):
-            cp = pone.tile([P, 4, 3, GT], F32, name="cp", tag="sm")
+            cp = pone.tile([P, 4, 3, GP], F32, name="cp", tag="sm")
             nc.tensor.matmul(
-                out=cp[:].rearrange("p j b i -> p (j b i)"),
-                lhsT=e8[:],
-                rhs=am_t[G][:].rearrange("p j c -> p (j c)"),
+                out=cp[:].rearrange("p j k c -> p (j k c)"),
+                lhsT=e4[:],
+                rhs=am_t[G][:].rearrange("p j f -> p (j f)"),
                 start=True,
                 stop=True,
             )
-            tmp = small.tile([P, GT, 4, 4], F32, name="tmp")
-            for k in range(3):
-                nc.vector.tensor_tensor(
-                    out=tmp[:, :, :, k + 1],
-                    in0=cp[:, :, k, :].rearrange("p j i -> p i j"),
-                    in1=wtab[:, :, k].unsqueeze(1).to_broadcast([P, GT, 4]),
-                    op=MULT,
-                )
+            tmp = small.tile([P, GP, 12], F32, name="tmp")
             nc.vector.tensor_tensor(
-                out=tmp[:, :, :, 0],
-                in0=a_t[G][:, 0, :].unsqueeze(2).to_broadcast([P, GT, 4]),
-                in1=wtab[:, :, 0].unsqueeze(1).to_broadcast([P, GT, 4]),
+                out=tmp[:],
+                in0=cp[:].rearrange("p j k c -> p c (j k)"),
+                in1=wtab[:].rearrange("p j k -> p (j k)").unsqueeze(1).to_broadcast([P, GP, 12]),
                 op=MULT,
             )
-            c = small.tile([P, GT * 4], F32, name="c")
-            nc.vector.tensor_reduce(out=c[:], in_=tmp[:].rearrange("p i j b -> p (i j) b"), axis=AX, op=ADD)
-            ct = small.tile([P, GT * 4, 16], F32, name="ct")
-            for k in range(0, GT * 4, 8):
+            cf = small.tile([P, GP * 4], F32, name="cf")
+            nc.vector.tensor_reduce(out=cf[:], in_=tmp[:].rearrange("p c (j k) -> p (c j) k", k=3), axis=AX, op=ADD)
+            mt = small.tile([P, GP, 32, 4], F32, name="mt")
+            for c in range(GP):
                 nc.gpsimd.tensor_tensor(
-                    out=ct[:, k : k + 8],
-                    in0=c[:, k : k + 8].unsqueeze(2).to_broadcast([P, 8, 16]),
-                    in1=bmask[:].unsqueeze(1).to_broadcast([P, 8, 16]),
+                    out=mt[:, c],
+                    in0=cf[:, 4 * c : 4 * c + 4].unsqueeze(1).to_broadcast([P, 32, 4]),
+                    in1=bmask[:].unsqueeze(2).to_broadcast([P, 32, 4]),
                     op=MULT,
                 )
-            ct_t[G] = ct
+            mt_t[G] = mt
 
-        def combine(i):
-            n, il = divmod(i, NT // B)
-            if il == 0:
-                db_t[n] = two.tile([P, 2, 512, 4], BF16, name="db", align_bytes=256)
-            db = db_t[n]
-            ct = ct_t[i // GT]
-            k4 = 4 * (i % GT)
-            dp = pxt.tile([P, 2, 4, 64], F32, name="dp", tag="tp")
-            for g in range(2):
-                for k in range(4):
-                    nc.tensor.matmul(
-                        out=dp[:, g, k, :],
-                        lhsT=h_t[i][:, g, k, :],
-                        rhs=ct[:, k4 : k4 + 4, :].rearrange("p t q -> p (t q)"),
-                        start=True,
-                        stop=True,
-                    )
-            for g in range(2):
+        def scale_e(c):
+            k = kap_t[c // GP][:, c % GP : c % GP + 1]
+            for half in range(2):
+                nc.scalar.activation(out=he_t[c][:, half, :], in_=he_t[c][:, half, :], func=COPY, scale=k)
+
+        def combine(c):
+            mt = mt_t[c // GP]
+            dsb = work.tile([P, 2, 2, P, 2], BF16, name="dsb", align_bytes=256)
+            d_t[c] = dsb
+            for half in range(2):
+                cols = slice(512 * half, 512 * (half + 1))
+                dp = pxt.tile([P, 512], F32, name="dp", tag="tp")
+                nc.tensor.matmul(out=dp[:], lhsT=ones[:], rhs=brow[:, cols], start=True, stop=False)
+                nc.tensor.matmul(
+                    out=dp[:], lhsT=mt[:, c % GP].rearrange("p q j -> p (q j)"), rhs=s_t[c][:, half, :],
+                    start=False, stop=True,
+                )
                 nc.vector.tensor_tensor(
-                    out=db[:, g].rearrange("p (t c) k -> p t c k", t=4)[:, :, 16 * il : 16 * il + 16, :],
-                    in0=dp[:, g].rearrange("p k (t q) -> p t q k", t=4),
-                    in1=b1t[:, g, :].unsqueeze(1).unsqueeze(1).to_broadcast([P, 4, 16, 4]),
+                    out=dsb[:, half],
+                    in0=dp[:].rearrange("p (r u e) -> p u r e", u=2, e=2),
+                    in1=he_t[c][:, half, :].rearrange("p (r u e) -> p u r e", u=2, e=2),
                     op=ADD,
                 )
 
-        dq_t = {}
+        def flip_d(c):
+            n, cl = divmod(c, NP // B)
+            if cl == 0:
+                db_t[n] = two.tile([P, 2, 512, 4], BF16, name="db", align_bytes=256)
+            xt = flip(d_t[c][:].bitcast(F32).rearrange("p g u r e -> p g u (r e)"))
+            for g in range(2):
+                nc.scalar.copy(
+                    out=db_t[n][:, g].bitcast(F32).rearrange("p (t c) u -> p t c u", t=4)[:, :, 32 * cl : 32 * cl + 32, :],
+                    in_=xt[:, g].rearrange("p u (q t) -> p t q u", t=4),
+                )
 
         def quant_d(n):
             dq = two.tile([P, 2, 512], U32, name="dq", align_bytes=256)
@@ -277,95 +326,142 @@ def tile_charformersoftsubwordblockmixer_x2_kernel(
                 )
             dq_t[n] = (dq, ds)
 
-        y_t = {}
-
-        def stage2(n, half, t):
+        def stage2(n, o0, pair):
             dq, ds = dq_t[n]
-            cols = slice(512 * half, 512 * (half + 1))
-            if t == 0:
-                y_t[n, half] = two.tile([P, 4, 512], F32, name="yf", align_bytes=256)
-            yf = y_t[n, half]
-            acc = pmm.tile([P, 512], F32, name="mm")
-            rows = slice(P * t, P * (t + 1))
-            for g in range(2):
-                nc.tensor.matmul_mx(
-                    out=acc[:],
-                    lhsT=dq[:, g, rows].bitcast(FP8X4),
-                    lhsT_scale=ds[:, g, rows],
-                    rhs=w2w[:, g, cols].bitcast(FP8X4),
-                    rhs_scale=w2s[:, g, cols],
-                    start=(g == 0),
-                    stop=(g == 1),
-                )
-            nc.scalar.copy(out=yf[:, t, :], in_=acc[:])
-            if t == 3:
+            cols = slice(o0, o0 + CW)
+            if pair == 0:
+                y_t[n, o0] = two.tile([P, 4, CW], F32, name="yf", align_bytes=256, bufs=4)
+            yf = y_t[n, o0]
+            acc = pmm.tile([P, 2, CW], F32, name="acc2", tag="mm")
+            for e in range(2):
+                t = 2 * pair + e
+                rows = slice(P * t, P * (t + 1))
+                for g in range(2):
+                    nc.tensor.matmul_mx(
+                        out=acc[:, e, :],
+                        lhsT=dq[:, g, rows].bitcast(FP8X4),
+                        lhsT_scale=ds[:, g, rows],
+                        rhs=w2w[:, g, cols].bitcast(FP8X4),
+                        rhs_scale=w2s[:, g, cols],
+                        start=(g == 0),
+                        stop=(g == 1),
+                    )
+            nc.scalar.copy(out=yf[:, 2 * pair : 2 * pair + 2, :], in_=acc[:])
+            if pair == 1:
                 nc.sync.dma_start(
                     out=out_0[n].rearrange("(p t) o -> p t o", t=4)[:, :, cols], in_=yf[:]
                 )
 
-        def planes_out(n, half):
-            yf = y_t[n, half]
-            yb = two.tile([P, 512, 4], BF16, name="yb", align_bytes=256)
-            nc.vector.tensor_copy(out=yb[:], in_=yf[:].rearrange("p t o -> p o t"))
-            yq = two.tile([P, 512], U32, name="yq", align_bytes=256)
-            ys = two.tile([P, 512], U8, name="ys", align_bytes=256)
+        def interleave(n, o0):
+            yb = two.tile([P, CW, 4], BF16, name="yb", align_bytes=256, bufs=4)
+            nc.vector.tensor_copy(out=yb[:], in_=y_t[n, o0][:].rearrange("p t o -> p o t"))
+            y_t[n, o0] = yb
+
+        def planes_out(n, o0):
+            yb = y_t[n, o0]
+            yq = two.tile([P, CW], U32, name="yq", align_bytes=256, bufs=4)
+            c0 = o0 % 512
+            if c0 == 0:
+                y_t[n, "s"] = two.tile([P, 512], U8, name="ys", align_bytes=256)
+            ys = y_t[n, "s"]
             nc.vector.quantize_mx(
-                out=yq[:].bitcast(FP8X4), scales=ys[:], in_=yb[:].rearrange("p o t -> p (o t)")
+                out=yq[:].bitcast(FP8X4), scales=ys[:, c0 : c0 + CW], in_=yb[:].rearrange("p o t -> p (o t)")
             )
-            m0 = n * DO + half * 512
+            m0 = n * DO + o0
             nc.sync.dma_start(
-                out=out_1[0].rearrange("p m t -> p (m t)")[:, 4 * m0 : 4 * (m0 + 512)].bitcast(I32),
+                out=out_1[0].rearrange("p m t -> p (m t)")[:, 4 * m0 : 4 * (m0 + CW)].bitcast(I32),
                 in_=yq[:].bitcast(I32),
             )
-            for q in range(4):
-                nc.sync.dma_start(
-                    out=out_2[0, 4 * q : 4 * q + 4, m0 : m0 + 512].bitcast(I32),
-                    in_=ys[32 * q : 32 * q + 4, :].bitcast(I32),
-                )
+            if c0 == 256:
+                m0 -= 256
+                for q in range(4):
+                    nc.sync.dma_start(
+                        out=out_2[0, 4 * q : 4 * q + 4, m0 : m0 + 512].bitcast(I32),
+                        in_=ys[32 * q : 32 * q + 4, :].bitcast(I32),
+                    )
 
-        transposes(0)
-        transposes(1)
-        quant_x(0)
-        quant_x(1)
-        for s in range(8):
-            a, b = 2 * s, 2 * s + 1
-            if s < 7:
-                transposes(a + 2)
-                transposes(b + 2)
-            if s == 4:
-                softmax(0, scores_pe(0))
-            stage1(a)
-            if s < 7:
-                quant_x(a + 2)
-            if s >= 5:
-                combine(2 * (s - 5))
-            stage1(b)
-            if s == 4:
+        flip_x(0, 0)
+        flip_x(0, 1)
+        quant_x(0, 0)
+        spread_ws()
+        quant_x(0, 1)
+        stage1(0, 0)
+        stage1(0, 1)
+        flip_x(1, 0)
+        flip_x(1, 1)
+        quant_x(1, 0)
+        quant_x(1, 1)
+        constants()
+        units = [(o0, pair) for o0 in range(0, DO, CW) for pair in range(2)]
+        for c in range(1, NP):
+            if c < NP - 1:
+                flip_x(c + 1, 0)
+                flip_x(c + 1, 1)
+            if c == 7:
+                flip_d(0)
+            if c == 4:
+                scores(0, [(0, (0,)), (0, (1,)), (1, (0,)), (1, (1,))])
+            if c == 5:
+                scale_e(0)
+            if c == 6:
+                scale_e(1)
+            if c == 7:
+                pair_sum(2)
+                scale_e(2)
+            stage1(c, 0)
+            if c < NP - 1:
+                quant_x(c + 1, 0)
+            stage1(c, 1)
+            if c == 4:
                 coef(0)
-            if s < 7:
-                quant_x(b + 2)
-            if 5 <= s < 7:
-                combine(2 * (s - 5) + 1)
-        softmax(1, scores_pe(1))
-        combine(5)
-        combine(6)
+            if c < NP - 1:
+                quant_x(c + 1, 1)
+            if 5 <= c < 7:
+                combine(c - 5)
+        combine(2)
+        flip_d(1)
+        scores(1, [(3, (0,)), (3, (1,)), (4, (0,)), (4, (1,))])
+        scale_e(3)
+        combine(3)
+        flip_d(2)
         coef(1)
-        combine(7)
+        scale_e(4)
+        flip_d(3)
         quant_d(0)
-        units = [(half, t) for half in range(2) for t in range(4)]
-        combine(8)
-        for half, t in units[:4]:
-            stage2(0, half, t)
-        for i in range(9, 16):
-            combine(i)
-            if i == 11:
-                planes_out(0, 0)
+        pair_sum(5)
+        scale_e(5)
+        combine(4)
+        for o0, pair in units[:2]:
+            stage2(0, o0, pair)
+        combine(5)
+        pair_sum(6)
+        scale_e(6)
+        flip_d(4)
+        interleave(0, 0)
+        for o0, pair in units[2:4]:
+            stage2(0, o0, pair)
+        flip_d(5)
+        pair_sum(7)
+        scale_e(7)
+        combine(6)
+        planes_out(0, 0)
+        interleave(0, CW)
+        for o0, pair in units[4:5]:
+            stage2(0, o0, pair)
+        combine(7)
+        planes_out(0, CW)
+        flip_d(6)
+        flip_d(7)
         quant_d(1)
-        for half, t in units[4:]:
-            stage2(0, half, t)
-        for half in range(2):
-            for t in range(4):
-                stage2(1, half, t)
-            if half == 0:
-                planes_out(0, 1)
-            planes_out(1, half)
+        for o0, pair in units[5:]:
+            stage2(0, o0, pair)
+        interleave(0, 2 * CW)
+        interleave(0, 3 * CW)
+        planes_out(0, 2 * CW)
+        for o0, pair in units:
+            stage2(1, o0, pair)
+            if pair == 1:
+                interleave(1, o0)
+                if o0 == 0:
+                    planes_out(0, 3 * CW)
+                planes_out(1, o0)

from contextlib import ExitStack

import concourse.mybir as mybir
from concourse.masks import make_identity

F32 = mybir.dt.float32
BF16 = mybir.dt.bfloat16
U32 = mybir.dt.uint32
I32 = mybir.dt.int32
U8 = mybir.dt.uint8
FP8X4 = mybir.dt.float8_e4m3fn_x4
MULT = mybir.AluOpType.mult
ADD = mybir.AluOpType.add
SUB = mybir.AluOpType.subtract
MAX = mybir.AluOpType.max
GE = mybir.AluOpType.is_ge
AX = mybir.AxisListType.X
AXY = mybir.AxisListType.XY
EXP = mybir.ActivationFunctionType.Exp
COPY = mybir.ActivationFunctionType.Copy

B, L, D, F, DO = 2, 1024, 1024, 1024, 1024
P = 128
NP = 8
GP = 4
CW = 256
FLOPS = 2 * B * L * D * F + 2 * B * (L // 2) * F * DO + 2 * 4 * B * L * F


def tile_charformersoftsubwordblockmixer_x2_kernel(
    tc, x, w1_words, w1_scales, b1, ws, w2_words, w2_scales, out_0, out_1, out_2
):
    nc = tc.nc
    with ExitStack() as ctx:
        keep = ctx.enter_context(tc.tile_pool(name="keep", bufs=1))
        xin = ctx.enter_context(tc.tile_pool(name="xin", bufs=8))
        work = ctx.enter_context(tc.tile_pool(name="work", bufs=3))
        hpool = ctx.enter_context(tc.tile_pool(name="hpool", bufs=8))
        small = ctx.enter_context(tc.tile_pool(name="small", bufs=2))
        two = ctx.enter_context(tc.tile_pool(name="two", bufs=2))
        pmm = ctx.enter_context(tc.psum_pool(name="pmm", bufs=4))
        pxt = ctx.enter_context(tc.psum_pool(name="pxt", bufs=3))
        pone = ctx.enter_context(tc.psum_pool(name="pone", bufs=1))

        ctx.enter_context(tc.manual_schedule())

        w1w = keep.tile([P, 2, F], U32, align_bytes=256, name="w1w")
        w1s = keep.tile([P, 2, F], U8, align_bytes=256, name="w1s")
        w2w = keep.tile([P, 2, DO], U32, align_bytes=256, name="w2w")
        w2s = keep.tile([P, 2, DO], U8, align_bytes=256, name="w2s")
        wsb = keep.tile([P, F], BF16, name="wsb")
        wrow = keep.tile([P, F], BF16, name="wrow")
        brow = keep.tile([P, F], BF16, name="brow")
        ones = keep.tile([P, P], BF16, name="ones")

        ident = keep.tile([P, P], F32, name="ident")
        make_identity(nc, ident[:])
        nc.vector.memset(w1s[:].bitcast(I32), 0)
        nc.vector.memset(wrow[:], 0.0)
        nc.vector.memset(brow[:], 0.0)
        nc.gpsimd.memset(ones[:], 1.0)
        nc.gpsimd.memset(w2s[:].bitcast(I32), 0)
        scr = keep.tile([P, 1], F32, name="scr")
        nc.vector.memset(scr[:], 0.0)
        scr2 = keep.tile([P, 1], F32, name="scr2")
        nc.scalar.activation(out=scr2[:], in_=scr[:], func=EXP)

        x_t = []

        def load_x(c):
            t = xin.tile([P, 2, D], BF16, name="xp", align_bytes=256)
            n, cl = divmod(c, NP // B)
            rows = x[n, 256 * cl : 256 * (cl + 1), :].rearrange("(p e) k -> p e k", e=2)
            if c == 0:
                for e in range(2):
                    nc.sync.dma_start(out=t[:, e, :], in_=rows[:, e, :])
            else:
                nc.sync.dma_start(out=t[:], in_=rows)
            x_t.append(t)

        def load_w(words, tile, c0, c1):
            v = words.rearrange("g p n t -> p g (n t)")
            nc.sync.dma_start(
                out=tile[:, :, c0:c1].bitcast(I32), in_=v[:, :, 4 * c0 : 4 * c1].bitcast(I32)
            )

        def load_s(scales, tile):
            for q in range(4):
                nc.sync.dma_start(
                    out=tile[32 * q : 32 * q + 4, :, :].bitcast(I32),
                    in_=scales[:, 4 * q : 4 * q + 4, :].rearrange("g q n -> q g n").bitcast(I32),
                )

        load_x(0)
        load_s(w1_scales, w1s)
        load_w(w1_words, w1w, 0, 512)
        load_w(w1_words, w1w, 512, 1024)
        nc.gpsimd.dma_start(out=wrow[0:1, :], in_=ws.unsqueeze(0))
        load_x(1)
        nc.gpsimd.dma_start(out=brow[0:1, :], in_=b1.unsqueeze(0))
        for c in range(2, NP):
            load_x(c)
        load_s(w2_scales, w2s)
        load_w(w2_words, w2w, 0, 512)
        load_w(w2_words, w2w, 512, 1024)

        pool_m = []
        for b in (1, 2, 4):
            m = keep.tile([P, P], F32, name="pm%d" % b)
            nc.gpsimd.memset(m[:], 0.5 / b)
            pat = [[-b, P // b], [0, b]]
            nc.gpsimd.affine_select(out=m[:], in_=m[:], compare_op=GE, fill=0.0, base=0, pattern=pat, channel_multiplier=1)
            pat = [[b, P // b], [0, b]]
            nc.gpsimd.affine_select(out=m[:], in_=m[:], compare_op=GE, fill=0.0, base=b - 1, pattern=pat, channel_multiplier=-1)
            pool_m.append(m)
        e4 = keep.tile([P, P], F32, name="e4")
        wtab = keep.tile([P, 4, 3], F32, name="wtab")
        pmask = keep.tile([P, 4], F32, name="pmask")
        bmask = keep.tile([P, 32], F32, name="bmask")

        def constants():
            nc.vector.tensor_scalar(out=e4[:], in0=pool_m[2][:], scalar1=8.0, scalar2=None, op0=MULT)
            for k in range(3):
                nc.vector.tensor_reduce(
                    out=wtab[:, :, k],
                    in_=pool_m[k][:].rearrange("p (q j) -> p j q", j=4),
                    axis=AX,
                    op=ADD,
                )
            nc.vector.tensor_scalar(out=pmask[:], in0=wtab[:, :, 0], scalar1=2.0, scalar2=None, op0=MULT)
            nc.vector.tensor_scalar(out=bmask[:], in0=pool_m[2][:, 0:P:4], scalar1=8.0, scalar2=None, op0=MULT)

        def spread_ws():
            for half in range(2):
                cols = slice(512 * half, 512 * (half + 1))
                acc = pmm.tile([P, 512], F32, name="accw", tag="mm")
                nc.tensor.matmul(out=acc[:], lhsT=ones[:], rhs=wrow[:, cols], start=True, stop=True)
                nc.scalar.copy(out=wsb[:, cols], in_=acc[:])

        xg_t, xq_t, he_t, s_t, u_t, mt_t, am_t, kap_t, d_t, db_t, dq_t, y_t = ({}, {}, {}, {}, {}, {}, {}, {}, {}, {}, {}, {})

        def flip(words):
            xt = pxt.tile([P, 2, 2, P], F32, name="xt", tag="tp")
            for g in range(2):
                for u in range(2):
                    nc.tensor.transpose(xt[:, g, u, :], words[:, g, u, :], ident[:])
            return xt

        def flip_x(c, e):
            xt = flip(x_t[c][:, e, :].bitcast(F32).rearrange("p (g r u) -> p g u r", g=2, u=2))
            xg = work.tile([P, 2, P, 4], BF16, name="xg", align_bytes=256)
            nc.scalar.copy(out=xg[:].bitcast(F32), in_=xt[:].rearrange("p g u r -> p g r u"))
            xg_t[c, e] = xg

        def quant_x(c, e):
            xq = work.tile([P, 2, P], U32, name="xq", align_bytes=256)
            xs = work.tile([P, 2, P], U8, name="xs", align_bytes=256)
            nc.vector.quantize_mx(
                out=xq[:].rearrange("p g r -> p (g r)").bitcast(FP8X4),
                scales=xs[:].rearrange("p g r -> p (g r)"),
                in_=xg_t[c, e][:].rearrange("p g r k -> p (g r k)"),
            )
            xq_t[c, e] = (xq, xs)

        def stage1(c, e):
            xq, xs = xq_t[c, e]
            if c % GP == 0 and e == 0:
                u_t[c // GP] = small.tile([P, GP, 2, 2], F32, name="u")
            u = u_t[c // GP]
            if e == 0:
                he_t[c] = hpool.tile([P, 2, 512], F32, name="he", align_bytes=256)
                s_t[c] = hpool.tile([P, 2, 512], F32, name="s", align_bytes=256)
            for half in range(2):
                cols = slice(512 * half, 512 * (half + 1))
                acc = pmm.tile([P, 512], F32, name="mm")
                for g in range(2):
                    nc.tensor.matmul_mx(
                        out=acc[:],
                        lhsT=xq[:, g, :].bitcast(FP8X4),
                        lhsT_scale=xs[:, g, :],
                        rhs=w1w[:, g, cols].bitcast(FP8X4),
                        rhs_scale=w1s[:, g, cols],
                        start=(g == 0),
                        stop=(g == 1),
                    )
                prod = work.tile([P, 512], F32, name="prod")
                nc.vector.scalar_tensor_tensor(
                    out=prod[:], in0=acc[:], scalar=1.0, in1=wsb[:, cols], op0=MULT, op1=MULT,
                    accum_out=u[:, c % GP, e, half : half + 1],
                )
                if e == 0:
                    nc.scalar.copy(out=he_t[c][:, half, :], in_=acc[:])
                else:
                    nc.scalar.copy(out=s_t[c][:, half, :], in_=acc[:])

        def pair_sum(c, halves=(0, 1)):
            for half in halves:
                nc.vector.tensor_tensor(
                    out=s_t[c][:, half, :], in0=s_t[c][:, half, :], in1=he_t[c][:, half, :], op=ADD
                )

        def scores(G, between):
            u = u_t[G]
            sp = pone.tile([P, 3, GP, 2, 2], F32, name="sp", tag="sm")
            for k in range(3):
                nc.tensor.matmul(
                    out=sp[:, k].rearrange("p c e h -> p (c e h)"),
                    lhsT=pool_m[k][:],
                    rhs=u[:].rearrange("p c e h -> p (c e h)"),
                    start=True,
                    stop=True,
                )
            lg = small.tile([P, 4, 2, GP], F32, name="lg")
            nc.vector.tensor_reduce(out=lg[:, 0].rearrange("p e c -> p c e"), in_=u[:], axis=AX, op=ADD)
            for e in range(2):
                nc.vector.tensor_reduce(out=lg[:, 1:4, e, :], in_=sp[:], axis=AXY, op=ADD)
            pair_sum(*between[0])
            mx = small.tile([P, 2 * GP], F32, name="mx")
            nc.vector.tensor_reduce(out=mx[:], in_=lg[:].rearrange("p b e c -> p (e c) b"), axis=AX, op=MAX)
            pair_sum(*between[1])
            sd = small.tile([P, 4, 2 * GP], F32, name="sd")
            nc.vector.tensor_tensor(
                out=sd[:], in0=lg[:].rearrange("p b e c -> p b (e c)"),
                in1=mx[:].unsqueeze(1).to_broadcast([P, 4, 2 * GP]), op=SUB,
            )
            ex = small.tile([P, 4, 2 * GP], F32, name="ex")
            nc.scalar.activation(out=ex[:], in_=sd[:], func=EXP)
            pair_sum(*between[2])
            sm = small.tile([P, 2 * GP], F32, name="sm")
            nc.vector.tensor_reduce(out=sm[:], in_=ex[:].rearrange("p b f -> p f b"), axis=AX, op=ADD)
            pair_sum(*between[3])
            rc = small.tile([P, 2 * GP], F32, name="rc")
            nc.vector.reciprocal(out=rc[:], in_=sm[:])
            a = small.tile([P, 4, 2, GP], F32, name="a")
            nc.vector.scalar_tensor_tensor(
                out=a[:].rearrange("p b e c -> p b (e c)"), in0=ex[:], scalar=0.5,
                in1=rc[:].unsqueeze(1).to_broadcast([P, 4, 2 * GP]), op0=MULT, op1=MULT,
            )
            ks = small.tile([P, 3, GP], F32, name="ks")
            nc.vector.tensor_tensor(out=ks[:], in0=a[:, 1:4, 0, :], in1=a[:, 1:4, 1, :], op=ADD)
            kap = small.tile([P, GP], F32, name="kap")
            nc.vector.tensor_tensor(out=kap[:], in0=a[:, 0, 0, :], in1=a[:, 0, 1, :], op=SUB)
            nc.vector.scalar_tensor_tensor(
                out=ks[:, 0, :], in0=a[:, 0, 1, :], scalar=2.0, in1=ks[:, 0, :], op0=MULT, op1=ADD
            )
            am = small.tile([P, 4, 3 * GP], F32, name="am")
            nc.vector.tensor_tensor(
                out=am[:],
                in0=ks[:].rearrange("p k c -> p (k c)").unsqueeze(1).to_broadcast([P, 4, 3 * GP]),
                in1=pmask[:].unsqueeze(2).to_broadcast([P, 4, 3 * GP]),
                op=MULT,
            )
            am_t[G], kap_t[G] = am, kap

        def coef(G):
            cp = pone.tile([P, 4, 3, GP], F32, name="cp", tag="sm")
            nc.tensor.matmul(
                out=cp[:].rearrange("p j k c -> p (j k c)"),
                lhsT=e4[:],
                rhs=am_t[G][:].rearrange("p j f -> p (j f)"),
                start=True,
                stop=True,
            )
            tmp = small.tile([P, GP, 12], F32, name="tmp")
            nc.vector.tensor_tensor(
                out=tmp[:],
                in0=cp[:].rearrange("p j k c -> p c (j k)"),
                in1=wtab[:].rearrange("p j k -> p (j k)").unsqueeze(1).to_broadcast([P, GP, 12]),
                op=MULT,
            )
            cf = small.tile([P, GP * 4], F32, name="cf")
            nc.vector.tensor_reduce(out=cf[:], in_=tmp[:].rearrange("p c (j k) -> p (c j) k", k=3), axis=AX, op=ADD)
            mt = small.tile([P, GP, 32, 4], F32, name="mt")
            for c in range(GP):
                nc.gpsimd.tensor_tensor(
                    out=mt[:, c],
                    in0=cf[:, 4 * c : 4 * c + 4].unsqueeze(1).to_broadcast([P, 32, 4]),
                    in1=bmask[:].unsqueeze(2).to_broadcast([P, 32, 4]),
                    op=MULT,
                )
            mt_t[G] = mt

        def scale_e(c):
            k = kap_t[c // GP][:, c % GP : c % GP + 1]
            for half in range(2):
                nc.scalar.activation(out=he_t[c][:, half, :], in_=he_t[c][:, half, :], func=COPY, scale=k)

        def combine(c):
            mt = mt_t[c // GP]
            dsb = work.tile([P, 2, 2, P, 2], BF16, name="dsb", align_bytes=256)
            d_t[c] = dsb
            for half in range(2):
                cols = slice(512 * half, 512 * (half + 1))
                dp = pxt.tile([P, 512], F32, name="dp", tag="tp")
                nc.tensor.matmul(out=dp[:], lhsT=ones[:], rhs=brow[:, cols], start=True, stop=False)
                nc.tensor.matmul(
                    out=dp[:], lhsT=mt[:, c % GP].rearrange("p q j -> p (q j)"), rhs=s_t[c][:, half, :],
                    start=False, stop=True,
                )
                nc.vector.tensor_tensor(
                    out=dsb[:, half],
                    in0=dp[:].rearrange("p (r u e) -> p u r e", u=2, e=2),
                    in1=he_t[c][:, half, :].rearrange("p (r u e) -> p u r e", u=2, e=2),
                    op=ADD,
                )

        def flip_d(c):
            n, cl = divmod(c, NP // B)
            if cl == 0:
                db_t[n] = two.tile([P, 2, 512, 4], BF16, name="db", align_bytes=256)
            xt = flip(d_t[c][:].bitcast(F32).rearrange("p g u r e -> p g u (r e)"))
            for g in range(2):
                nc.scalar.copy(
                    out=db_t[n][:, g].bitcast(F32).rearrange("p (t c) u -> p t c u", t=4)[:, :, 32 * cl : 32 * cl + 32, :],
                    in_=xt[:, g].rearrange("p u (q t) -> p t q u", t=4),
                )

        def quant_d(n):
            dq = two.tile([P, 2, 512], U32, name="dq", align_bytes=256)
            ds = two.tile([P, 2, 512], U8, name="ds", align_bytes=256)
            for g in range(2):
                nc.vector.quantize_mx(
                    out=dq[:, g, :].bitcast(FP8X4),
                    scales=ds[:, g, :],
                    in_=db_t[n][:, g].rearrange("p c k -> p (c k)"),
                )
            dq_t[n] = (dq, ds)

        def stage2(n, o0, pair):
            dq, ds = dq_t[n]
            cols = slice(o0, o0 + CW)
            if pair == 0:
                y_t[n, o0] = two.tile([P, 4, CW], F32, name="yf", align_bytes=256, bufs=4)
            yf = y_t[n, o0]
            acc = pmm.tile([P, 2, CW], F32, name="acc2", tag="mm")
            for e in range(2):
                t = 2 * pair + e
                rows = slice(P * t, P * (t + 1))
                for g in range(2):
                    nc.tensor.matmul_mx(
                        out=acc[:, e, :],
                        lhsT=dq[:, g, rows].bitcast(FP8X4),
                        lhsT_scale=ds[:, g, rows],
                        rhs=w2w[:, g, cols].bitcast(FP8X4),
                        rhs_scale=w2s[:, g, cols],
                        start=(g == 0),
                        stop=(g == 1),
                    )
            nc.scalar.copy(out=yf[:, 2 * pair : 2 * pair + 2, :], in_=acc[:])
            if pair == 1:
                nc.sync.dma_start(
                    out=out_0[n].rearrange("(p t) o -> p t o", t=4)[:, :, cols], in_=yf[:]
                )

        def interleave(n, o0):
            yb = two.tile([P, CW, 4], BF16, name="yb", align_bytes=256, bufs=4)
            nc.vector.tensor_copy(out=yb[:], in_=y_t[n, o0][:].rearrange("p t o -> p o t"))
            y_t[n, o0] = yb

        def planes_out(n, o0):
            yb = y_t[n, o0]
            yq = two.tile([P, CW], U32, name="yq", align_bytes=256, bufs=4)
            c0 = o0 % 512
            if c0 == 0:
                y_t[n, "s"] = two.tile([P, 512], U8, name="ys", align_bytes=256)
            ys = y_t[n, "s"]
            nc.vector.quantize_mx(
                out=yq[:].bitcast(FP8X4), scales=ys[:, c0 : c0 + CW], in_=yb[:].rearrange("p o t -> p (o t)")
            )
            m0 = n * DO + o0
            nc.sync.dma_start(
                out=out_1[0].rearrange("p m t -> p (m t)")[:, 4 * m0 : 4 * (m0 + CW)].bitcast(I32),
                in_=yq[:].bitcast(I32),
            )
            if c0 == 256:
                m0 -= 256
                for q in range(4):
                    nc.sync.dma_start(
                        out=out_2[0, 4 * q : 4 * q + 4, m0 : m0 + 512].bitcast(I32),
                        in_=ys[32 * q : 32 * q + 4, :].bitcast(I32),
                    )

        flip_x(0, 0)
        flip_x(0, 1)
        quant_x(0, 0)
        spread_ws()
        quant_x(0, 1)
        stage1(0, 0)
        stage1(0, 1)
        flip_x(1, 0)
        flip_x(1, 1)
        quant_x(1, 0)
        quant_x(1, 1)
        constants()
        units = [(o0, pair) for o0 in range(0, DO, CW) for pair in range(2)]
        for c in range(1, NP):
            if c < NP - 1:
                flip_x(c + 1, 0)
                flip_x(c + 1, 1)
            if c == 7:
                flip_d(0)
            if c == 4:
                scores(0, [(0, (0,)), (0, (1,)), (1, (0,)), (1, (1,))])
            if c == 5:
                scale_e(0)
            if c == 6:
                scale_e(1)
            if c == 7:
                pair_sum(2)
                scale_e(2)
            stage1(c, 0)
            if c < NP - 1:
                quant_x(c + 1, 0)
            stage1(c, 1)
            if c == 4:
                coef(0)
            if c < NP - 1:
                quant_x(c + 1, 1)
            if 5 <= c < 7:
                combine(c - 5)
        combine(2)
        flip_d(1)
        scores(1, [(3, (0,)), (3, (1,)), (4, (0,)), (4, (1,))])
        scale_e(3)
        combine(3)
        flip_d(2)
        coef(1)
        scale_e(4)
        flip_d(3)
        quant_d(0)
        pair_sum(5)
        scale_e(5)
        combine(4)
        for o0, pair in units[:2]:
            stage2(0, o0, pair)
        combine(5)
        pair_sum(6)
        scale_e(6)
        flip_d(4)
        interleave(0, 0)
        for o0, pair in units[2:4]:
            stage2(0, o0, pair)
        flip_d(5)
        pair_sum(7)
        scale_e(7)
        combine(6)
        planes_out(0, 0)
        interleave(0, CW)
        for o0, pair in units[4:5]:
            stage2(0, o0, pair)
        combine(7)
        planes_out(0, CW)
        flip_d(6)
        flip_d(7)
        quant_d(1)
        for o0, pair in units[5:]:
            stage2(0, o0, pair)
        interleave(0, 2 * CW)
        interleave(0, 3 * CW)
        planes_out(0, 2 * CW)
        for o0, pair in units:
            stage2(1, o0, pair)
            if pair == 1:
                interleave(1, o0)
                if o0 == 0:
                    planes_out(0, 3 * CW)
                planes_out(1, o0)
